import numpy as np
import ml_dtypes


def mxq(x, axis, fmt="e4m3"):
    dtype, down = {"e4m3": (ml_dtypes.float8_e4m3fn, 7), "e5m2": (ml_dtypes.float8_e5m2, 14)}[fmt]
    v = np.moveaxis(np.asarray(x, np.float32).astype(ml_dtypes.bfloat16).astype(np.float64), axis, -1)
    blocks = v.reshape(v.shape[:-1] + (-1, 32))
    amax = np.abs(blocks).max(-1, keepdims=True)
    byte = np.maximum(np.where(amax > 0, np.frexp(amax)[1] - 1 + 127, 0) - down, 1)
    scale = np.exp2(byte - 127.0)
    codes = (blocks / scale).astype(np.float32).astype(dtype).astype(np.float64)
    return np.moveaxis((codes * scale).reshape(v.shape), -1, axis)


WIDE = False


def mx_kscale(k):
    if not WIDE:
        return np.ones(k)
    levels = np.array([10, -10, 5, -5, 0])
    if k % 512:
        return np.exp2(np.random.permutation(np.resize(levels, k // 32))).repeat(32)
    a = np.empty((k // 512, 16))
    for p in range(k // 512):
        a[p, :8] = np.random.permutation(np.resize(levels, 8))
        for g in range(8):
            far = levels[np.abs(levels - a[p, g]) >= 10]
            a[p, g + 8] = far[np.random.randint(len(far))]
    return np.exp2(a.ravel()).repeat(32)


def f64(x):
    return np.asarray(x).astype(np.float64)


def striped(idx):
    return np.tile(idx.reshape(-1, 16).T, (8, 1)).astype(np.uint16)


def unstriped(offs):
    return offs[:16].T.reshape(-1).astype(np.int64)


def silu(v):
    return v / (1.0 + np.exp(-np.maximum(v, -700.0)))


K, T, E, C, H, N = 512, 2048, 16, 128, 512, 256


def by_expert(wq, xq):
    return np.concatenate([wq[e].T @ xq[:, e * C:(e + 1) * C] for e in range(E)], axis=1)


def setup_inputs():
    n = np.random.standard_normal
    s = mx_kscale(K)[:, None]
    u = mx_kscale(H)
    return {
        "xT": (n((K, T)) * s).astype(np.float32),
        "w1": (n((E, K, H)) / np.sqrt(K) / s[None] * u[None, None, :]).astype(np.float32),
        "w2": (n((E, H, N)) / np.sqrt(H) / u[None, :, None]).astype(np.float32),
        "gate": np.tile(np.random.uniform(0.2, 1.0, E * C), (N, 1)).astype(np.float32),
        "offs": striped(np.random.permutation(T)[:E * C]),
    }


def reference(xT, w1, w2, gate, offs):
    idx = unstriped(offs)
    xq = mxq(f64(xT)[:, idx], 0, "e4m3")
    h = silu(by_expert(mxq(f64(w1), 1, "e4m3"), xq))
    y = by_expert(mxq(f64(w2), 1, "e4m3"), mxq(h, 0, "e4m3"))
    out = np.zeros((N, T))
    out[:, idx] = f64(gate) * y
    return out

@@ -1,0 +1,157 @@
+from contextlib import ExitStack
+
+import concourse.mybir as mybir
+from concourse.masks import make_identity
+
+K, T, E, C, H, N = 512, 2048, 16, 128, 512, 256
+FLOPS = 2 * E * C * (K * H + H * N)
+BYTES = 4 * (K * T + E * K * H + E * H * N + N * T + 8 * E * C) + 2 * 128 * (E * C // 16)
+
+F32 = mybir.dt.float32
+BF16 = mybir.dt.bfloat16
+U32 = mybir.dt.uint32
+U16 = mybir.dt.uint16
+U8 = mybir.dt.uint8
+FP8X4 = mybir.dt.float8_e4m3fn_x4
+SILU = mybir.ActivationFunctionType.Silu
+MULT = mybir.AluOpType.mult
+
+P = 128
+PACK = 4
+PAIR = 2 * C
+X_CHUNKS = (256, 256, 512, 512, 512)
+X_VECTOR = 5
+
+
+def tile_routed_moe_kernel(tc, xT, w1, w2, gate, offs, out):
+    nc = tc.nc
+    with ExitStack() as ctx:
+        keep = ctx.enter_context(tc.tile_pool(name="keep", bufs=1))
+        raws = ctx.enter_context(tc.tile_pool(name="raws", bufs=13))
+        stage = ctx.enter_context(tc.tile_pool(name="stage", bufs=6))
+        codes = ctx.enter_context(tc.tile_pool(name="codes", bufs=4))
+        psum = ctx.enter_context(tc.psum_pool(name="psum", bufs=3))
+        gpsum = ctx.enter_context(tc.psum_pool(name="gpsum", bufs=2))
+
+        offsets = keep.tile([P, T // 16], U16, name="offsets")
+        x_words = keep.tile([P, T], U32, name="x_words", align_bytes=64)
+        x_scales = keep.tile([P, T], U8, name="x_scales", align_bytes=64)
+        gate_rows = keep.tile([P, C], F32, name="gate_rows")
+        gates = keep.tile([P, E * C], F32, name="gates")
+        ident = keep.tile([P, P], F32, name="ident")
+        window0 = keep.tile([P, T], F32, name="window0")
+        window1 = keep.tile([P, T], F32, name="window1")
+        windows = [window0, window1]
+
+        nc.gpsimd.memset(x_scales[:], 0)
+        make_identity(nc, ident[:])
+
+        xT_planes = xT.rearrange("(p j) t -> p j t", j=PACK)
+        t0 = 0
+        for index, width in enumerate(X_CHUNKS):
+            cols = slice(t0, t0 + width)
+            raw = raws.tile([P, PACK, width], F32, name="x_raw", tag="raw")
+            nc.sync.dma_start(out=raw[:], in_=xT_planes[:, :, cols])
+            if index == 0:
+                nc.sync.dma_start(out=gate_rows[:], in_=gate[0:8, :].rearrange("r (e c) -> (r e) c", c=C))
+            if index == 1:
+                nc.sync.dma_start(offsets[:], offs)
+            grouped = stage.tile([P, width * PACK], BF16, name="x_grouped", tag="grouped", align_bytes=64)
+            dst = grouped[:].rearrange("p (c i j) -> p c j i", i=4, j=PACK)
+            src = raw[:].rearrange("p j (c i) -> p c j i", i=4)
+            cut = (width // 4) * X_VECTOR // 8
+            nc.vector.tensor_copy(out=dst[:, :cut], in_=src[:, :cut])
+            nc.scalar.copy(out=dst[:, cut:], in_=src[:, cut:])
+            nc.vector.quantize_mx(out=x_words[:, cols].bitcast(FP8X4), scales=x_scales[:, cols], in_=grouped[:])
+            t0 += width
+
+        for quad in range(E // 4):
+            bank = gpsum.tile([P, 4, C], F32, name="gate_bank")
+            for i in range(4):
+                e = 4 * quad + i
+                nc.tensor.matmul(bank[:, i, :], ident[:, e : e + 1].to_broadcast([P, P]), gate_rows[:], start=True, stop=True)
+            nc.scalar.copy(out=gates[:, 512 * quad : 512 * quad + 512], in_=bank[:].rearrange("p i c -> p (i c)"))
+
+        for q in range(E // 2):
+            last = q == E // 2 - 1
+            slots = slice(PAIR * q, PAIR * (q + 1))
+            index_cols = offsets[:, slots.start // 16 : slots.stop // 16]
+
+            w1_words = []
+            w1_scales = []
+            for e in (2 * q, 2 * q + 1):
+                raw = raws.tile([P, PACK, H], F32, name="w1_raw", tag="raw")
+                nc.sync.dma_start(out=raw[:], in_=w1[e].rearrange("(p j) i -> p j i", j=PACK))
+                grouped = stage.tile([P, H * PACK], BF16, name="w1_grouped", tag="grouped", align_bytes=64)
+                dst = grouped[:].rearrange("p (t m j) -> p m j t", t=4, j=PACK)
+                src = raw[:].rearrange("p j (m t) -> p m j t", t=4)
+                nc.scalar.copy(out=dst[:, :64], in_=src[:, :64])
+                if last:
+                    nc.vector.tensor_copy(out=dst[:, 64:], in_=src[:, 64:])
+                else:
+                    nc.scalar.copy(out=dst[:, 64:], in_=src[:, 64:])
+                words = codes.tile([P, H], U32, name="w1_words", align_bytes=64)
+                scales = codes.tile([P, H], U8, name="w1_scales", align_bytes=64)
+                nc.vector.quantize_mx(out=words[:].bitcast(FP8X4), scales=scales[:], in_=grouped[:])
+                w1_words.append(words)
+                w1_scales.append(scales)
+            raw = raws.tile([P, 2, PACK, N], F32, name="w2_raw", tag="raw")
+            nc.sync.dma_start(out=raw[:], in_=w2[2 * q : 2 * q + 2].rearrange("e (p j) n -> p e j n", j=PACK))
+            grouped = stage.tile([P, 2 * N * PACK], BF16, name="w2_grouped", tag="grouped", align_bytes=64)
+            dst = grouped[:].rearrange("p (e c i j) -> p e c j i", e=2, i=4, j=PACK)
+            src = raw[:].rearrange("p e j (c i) -> p e c j i", i=4)
+            nc.vector.tensor_copy(out=dst[:, 0], in_=src[:, 0])
+            nc.scalar.copy(out=dst[:, 1], in_=src[:, 1])
+            w2_words = codes.tile([P, 2 * N], U32, name="w2_words", align_bytes=64)
+            w2_scales = codes.tile([P, 2 * N], U8, name="w2_scales", align_bytes=64)
+            nc.vector.quantize_mx(out=w2_words[:].bitcast(FP8X4), scales=w2_scales[:], in_=grouped[:])
+
+            slot_words = codes.tile([P, PAIR], U32, name="slot_words", align_bytes=64)
+            slot_scales = codes.tile([P, PAIR], U8, name="slot_scales", align_bytes=64)
+            nc.vector.tensor_copy(slot_words[:], x_words[:].indirect(index_cols))
+            nc.vector.tensor_copy(slot_scales[:], x_scales[:].indirect(index_cols))
+
+            h_words = codes.tile([P, PAIR], U32, name="h_words", align_bytes=64)
+            h_scales = codes.tile([P, PAIR], U8, name="h_scales", align_bytes=64)
+            for i in range(2):
+                mine = slice(C * i, C * (i + 1))
+                h_bank = psum.tile([P, 4, C], F32, name="h_bank")
+                for t in range(4):
+                    nc.tensor.matmul_mx(
+                        out=h_bank[:, t, :],
+                        lhsT=w1_words[i][:, P * t : P * (t + 1)].bitcast(FP8X4),
+                        lhsT_scale=w1_scales[i][:, P * t : P * (t + 1)],
+                        rhs=slot_words[:, mine].bitcast(FP8X4),
+                        rhs_scale=slot_scales[:, mine],
+                        start=True,
+                        stop=True,
+                    )
+                hidden = codes.tile([P, C * PACK], BF16, name="hidden", align_bytes=64)
+                nc.scalar.activation(
+                    out=hidden[:].rearrange("p (c t) -> p c t", t=PACK),
+                    in_=h_bank[:].rearrange("p t c -> p c t"),
+                    func=SILU,
+                )
+                nc.vector.quantize_mx(out=h_words[:, mine].bitcast(FP8X4), scales=h_scales[:, mine], in_=hidden[:])
+
+            y_bank = psum.tile([P, 2, PAIR], F32, name="y_bank")
+            for b in range(2):
+                for i in range(2):
+                    mine = slice(C * i, C * (i + 1))
+                    rows = slice(N * i + P * b, N * i + P * (b + 1))
+                    nc.tensor.matmul_mx(
+                        out=y_bank[:, b, mine],
+                        lhsT=w2_words[:, rows].bitcast(FP8X4),
+                        lhsT_scale=w2_scales[:, rows],
+                        rhs=h_words[:, mine].bitcast(FP8X4),
+                        rhs_scale=h_scales[:, mine],
+                        start=True,
+                        stop=True,
+                    )
+            for b in range(2):
+                gated = codes.tile([P, PAIR], F32, name="gated")
+                nc.vector.tensor_tensor(gated[:], y_bank[:, b, :], gates[:, slots], MULT)
+                nc.vector.tensor_copy(windows[b][:].indirect(index_cols), gated[:])
+
+        for b in range(2):
+            nc.sync.dma_start(out=out[P * b : P * (b + 1), :], in_=windows[b][:])

@@ -5,7 +5,8 @@ from concourse.masks import make_identity
 
 K, T, E, C, H, N = 512, 2048, 16, 128, 512, 256
 FLOPS = 2 * E * C * (K * H + H * N)
-BYTES = 4 * (K * T + E * K * H + E * H * N + N * T + 8 * E * C) + 2 * 128 * (E * C // 16)
+GATE_ROWS = 8
+BYTES = 4 * (K * T + E * K * H + E * H * N + N * T + GATE_ROWS * E * C) + 2 * 128 * (E * C // 16)
 
 F32 = mybir.dt.float32
 BF16 = mybir.dt.bfloat16
@@ -14,24 +15,28 @@ U16 = mybir.dt.uint16
 U8 = mybir.dt.uint8
 FP8X4 = mybir.dt.float8_e4m3fn_x4
 SILU = mybir.ActivationFunctionType.Silu
+IDENTITY = mybir.ActivationFunctionType.Identity
 MULT = mybir.AluOpType.mult
 
 P = 128
 PACK = 4
+PAIRS = E // 2
 PAIR = 2 * C
-X_CHUNKS = (256, 256, 512, 512, 512)
-X_VECTOR = 5
+X_CHUNKS = (256, 512, 512, 512, 256)
+GATHERS = {0: 1, 1: 1, 2: 1, 3: 1, 4: 2, 6: 2}
+W1_PIECES = (64, 32, 32)
 
 
 def tile_routed_moe_kernel(tc, xT, w1, w2, gate, offs, out):
     nc = tc.nc
     with ExitStack() as ctx:
         keep = ctx.enter_context(tc.tile_pool(name="keep", bufs=1))
-        raws = ctx.enter_context(tc.tile_pool(name="raws", bufs=13))
-        stage = ctx.enter_context(tc.tile_pool(name="stage", bufs=6))
-        codes = ctx.enter_context(tc.tile_pool(name="codes", bufs=4))
+        raws = ctx.enter_context(tc.tile_pool(name="raws", bufs=12))
+        stage = ctx.enter_context(tc.tile_pool(name="stage", bufs=4))
+        codes = ctx.enter_context(tc.tile_pool(name="codes", bufs=3))
+        sums_pool = ctx.enter_context(tc.tile_pool(name="sums_pool", bufs=3))
         psum = ctx.enter_context(tc.psum_pool(name="psum", bufs=3))
-        gpsum = ctx.enter_context(tc.psum_pool(name="gpsum", bufs=2))
+        gate_psum = ctx.enter_context(tc.psum_pool(name="gate_psum", bufs=2))
 
         offsets = keep.tile([P, T // 16], U16, name="offsets")
         x_words = keep.tile([P, T], U32, name="x_words", align_bytes=64)
@@ -39,101 +44,140 @@ def tile_routed_moe_kernel(tc, xT, w1, w2, gate, offs, out):
         gate_rows = keep.tile([P, C], F32, name="gate_rows")
         gates = keep.tile([P, E * C], F32, name="gates")
         ident = keep.tile([P, P], F32, name="ident")
+        zeros = keep.tile([P, 2 * E], F32, name="zeros")
         window0 = keep.tile([P, T], F32, name="window0")
         window1 = keep.tile([P, T], F32, name="window1")
         windows = [window0, window1]
 
+        nc.vector.memset(zeros[:, 0:1], 0.0)
+        nc.scalar.activation(out=zeros[:, 1:2], in_=zeros[:, 0:1], func=SILU)
         nc.gpsimd.memset(x_scales[:], 0)
         make_identity(nc, ident[:])
 
-        xT_planes = xT.rearrange("(p j) t -> p j t", j=PACK)
-        t0 = 0
-        for index, width in enumerate(X_CHUNKS):
-            cols = slice(t0, t0 + width)
+        xT_rows = xT.rearrange("(p j) t -> p j t", j=PACK)
+        x_raw = []
+        start = 0
+        for k, width in enumerate(X_CHUNKS):
             raw = raws.tile([P, PACK, width], F32, name="x_raw", tag="raw")
-            nc.sync.dma_start(out=raw[:], in_=xT_planes[:, :, cols])
-            if index == 0:
-                nc.sync.dma_start(out=gate_rows[:], in_=gate[0:8, :].rearrange("r (e c) -> (r e) c", c=C))
-            if index == 1:
+            nc.sync.dma_start(out=raw[:], in_=xT_rows[:, :, start : start + width])
+            x_raw.append(raw)
+            start += width
+            if k == 0:
+                nc.sync.dma_start(out=gate_rows[:], in_=gate[0:GATE_ROWS, :].rearrange("r (e c) -> (r e) c", c=C))
+            if k == 1:
                 nc.sync.dma_start(offsets[:], offs)
-            grouped = stage.tile([P, width * PACK], BF16, name="x_grouped", tag="grouped", align_bytes=64)
+
+        start = 0
+        for k, width in enumerate(X_CHUNKS):
+            cols = slice(start, start + width)
+            start += width
+            grouped = stage.tile([P, width * PACK], BF16, name="x_grouped", align_bytes=64)
             dst = grouped[:].rearrange("p (c i j) -> p c j i", i=4, j=PACK)
-            src = raw[:].rearrange("p j (c i) -> p c j i", i=4)
-            cut = (width // 4) * X_VECTOR // 8
+            src = x_raw[k][:].rearrange("p j (c i) -> p c j i", i=4)
+            cut = (width // 4) * 3 // 4
             nc.vector.tensor_copy(out=dst[:, :cut], in_=src[:, :cut])
             nc.scalar.copy(out=dst[:, cut:], in_=src[:, cut:])
             nc.vector.quantize_mx(out=x_words[:, cols].bitcast(FP8X4), scales=x_scales[:, cols], in_=grouped[:])
-            t0 += width
 
         for quad in range(E // 4):
-            bank = gpsum.tile([P, 4, C], F32, name="gate_bank")
+            bank = gate_psum.tile([P, 4, C], F32, name="gate_bank")
             for i in range(4):
                 e = 4 * quad + i
                 nc.tensor.matmul(bank[:, i, :], ident[:, e : e + 1].to_broadcast([P, P]), gate_rows[:], start=True, stop=True)
-            nc.scalar.copy(out=gates[:, 512 * quad : 512 * quad + 512], in_=bank[:].rearrange("p i c -> p (i c)"))
+            nc.scalar.copy(out=gates[:, 4 * C * quad : 4 * C * (quad + 1)], in_=bank[:].rearrange("p i c -> p (i c)"))
 
-        for q in range(E // 2):
-            last = q == E // 2 - 1
-            slots = slice(PAIR * q, PAIR * (q + 1))
-            index_cols = offsets[:, slots.start // 16 : slots.stop // 16]
+        w1_grouped, w2_grouped, w1_codes, w2_codes = {}, {}, {}, {}
+        slot_codes, hidden_of, h_codes, sums_of = {}, {}, {}, {}
 
-            w1_words = []
-            w1_scales = []
+        def zero_of(e):
+            return zeros[:, E + e : E + e + 1] if e < E else 0.0
+
+        def convert_w1(q):
             for e in (2 * q, 2 * q + 1):
                 raw = raws.tile([P, PACK, H], F32, name="w1_raw", tag="raw")
                 nc.sync.dma_start(out=raw[:], in_=w1[e].rearrange("(p j) i -> p j i", j=PACK))
-                grouped = stage.tile([P, H * PACK], BF16, name="w1_grouped", tag="grouped", align_bytes=64)
+                grouped = stage.tile([P, H * PACK], BF16, name="w1_grouped", align_bytes=64)
                 dst = grouped[:].rearrange("p (t m j) -> p m j t", t=4, j=PACK)
                 src = raw[:].rearrange("p j (m t) -> p m j t", t=4)
-                nc.scalar.copy(out=dst[:, :64], in_=src[:, :64])
-                if last:
-                    nc.vector.tensor_copy(out=dst[:, 64:], in_=src[:, 64:])
-                else:
-                    nc.scalar.copy(out=dst[:, 64:], in_=src[:, 64:])
-                words = codes.tile([P, H], U32, name="w1_words", align_bytes=64)
-                scales = codes.tile([P, H], U8, name="w1_scales", align_bytes=64)
-                nc.vector.quantize_mx(out=words[:].bitcast(FP8X4), scales=scales[:], in_=grouped[:])
-                w1_words.append(words)
-                w1_scales.append(scales)
+                m = 0
+                for k, width in enumerate(W1_PIECES):
+                    nc.scalar.copy(out=dst[:, m : m + width], in_=src[:, m : m + width])
+                    m += width
+                    if k == 1:
+                        nc.scalar.mul(zeros[:, E + e : E + e + 1], grouped[:, 0:1], 0.0)
+                w1_grouped[e] = grouped
+
+        def convert_w2(q):
             raw = raws.tile([P, 2, PACK, N], F32, name="w2_raw", tag="raw")
             nc.sync.dma_start(out=raw[:], in_=w2[2 * q : 2 * q + 2].rearrange("e (p j) n -> p e j n", j=PACK))
-            grouped = stage.tile([P, 2 * N * PACK], BF16, name="w2_grouped", tag="grouped", align_bytes=64)
+            grouped = stage.tile([P, 2 * N * PACK], BF16, name="w2_grouped", align_bytes=64, bufs=1)
             dst = grouped[:].rearrange("p (e c i j) -> p e c j i", e=2, i=4, j=PACK)
             src = raw[:].rearrange("p e j (c i) -> p e c j i", i=4)
-            nc.vector.tensor_copy(out=dst[:, 0], in_=src[:, 0])
-            nc.scalar.copy(out=dst[:, 1], in_=src[:, 1])
-            w2_words = codes.tile([P, 2 * N], U32, name="w2_words", align_bytes=64)
-            w2_scales = codes.tile([P, 2 * N], U8, name="w2_scales", align_bytes=64)
-            nc.vector.quantize_mx(out=w2_words[:].bitcast(FP8X4), scales=w2_scales[:], in_=grouped[:])
-
-            slot_words = codes.tile([P, PAIR], U32, name="slot_words", align_bytes=64)
-            slot_scales = codes.tile([P, PAIR], U8, name="slot_scales", align_bytes=64)
-            nc.vector.tensor_copy(slot_words[:], x_words[:].indirect(index_cols))
-            nc.vector.tensor_copy(slot_scales[:], x_scales[:].indirect(index_cols))
-
-            h_words = codes.tile([P, PAIR], U32, name="h_words", align_bytes=64)
-            h_scales = codes.tile([P, PAIR], U8, name="h_scales", align_bytes=64)
             for i in range(2):
-                mine = slice(C * i, C * (i + 1))
+                nc.vector.tensor_copy(out=dst[:, i], in_=src[:, i])
+            w2_grouped[q] = grouped
+
+        def quantize_w1(q):
+            for e in (2 * q, 2 * q + 1):
+                words = codes.tile([P, H], U32, name="w1_words", align_bytes=64)
+                scales = codes.tile([P, H], U8, name="w1_scales", align_bytes=64)
+                nc.vector.quantize_mx(out=words[:].bitcast(FP8X4), scales=scales[:], in_=w1_grouped[e][:])
+                w1_codes[e] = (words, scales)
+
+        def quantize_w2(q):
+            words = codes.tile([P, 2 * N], U32, name="w2_words", align_bytes=64)
+            scales = codes.tile([P, 2 * N], U8, name="w2_scales", align_bytes=64)
+            nc.vector.quantize_mx(out=words[:].bitcast(FP8X4), scales=scales[:], in_=w2_grouped[q][:])
+            w2_codes[q] = (words, scales)
+
+        def gather_tokens(q):
+            if q not in GATHERS:
+                return
+            n = GATHERS[q]
+            index_cols = offsets[:, PAIR // 16 * q : PAIR // 16 * (q + n)]
+            words = codes.tile([P, n * PAIR], U32, name="slot_words", align_bytes=64, bufs=4)
+            scales = codes.tile([P, n * PAIR], U8, name="slot_scales", align_bytes=64, bufs=4)
+            nc.vector.tensor_copy(words[:], x_words[:].indirect(index_cols))
+            nc.vector.tensor_copy(scales[:], x_scales[:].indirect(index_cols))
+            for k in range(n):
+                slot_codes[q + k] = (words, scales, PAIR * k)
+
+        def layer_one(q):
+            slot_words, slot_scales, base = slot_codes[q]
+            hidden = stage.tile([P, PAIR * PACK], BF16, name="hidden", align_bytes=64, bufs=2)
+            for i in range(2):
+                e = 2 * q + i
+                words, scales = w1_codes[e]
+                mine = slice(base + C * i, base + C * (i + 1))
                 h_bank = psum.tile([P, 4, C], F32, name="h_bank")
                 for t in range(4):
+                    rows = slice(P * t, P * (t + 1))
                     nc.tensor.matmul_mx(
                         out=h_bank[:, t, :],
-                        lhsT=w1_words[i][:, P * t : P * (t + 1)].bitcast(FP8X4),
-                        lhsT_scale=w1_scales[i][:, P * t : P * (t + 1)],
+                        lhsT=words[:, rows].bitcast(FP8X4),
+                        lhsT_scale=scales[:, rows],
                         rhs=slot_words[:, mine].bitcast(FP8X4),
                         rhs_scale=slot_scales[:, mine],
                         start=True,
                         stop=True,
                     )
-                hidden = codes.tile([P, C * PACK], BF16, name="hidden", align_bytes=64)
                 nc.scalar.activation(
-                    out=hidden[:].rearrange("p (c t) -> p c t", t=PACK),
+                    out=hidden[:, PACK * C * i : PACK * C * (i + 1)].rearrange("p (c t) -> p c t", t=PACK),
                     in_=h_bank[:].rearrange("p t c -> p c t"),
                     func=SILU,
+                    bias=zero_of(e + 1),
                 )
-                nc.vector.quantize_mx(out=h_words[:, mine].bitcast(FP8X4), scales=h_scales[:, mine], in_=hidden[:])
+            hidden_of[q] = hidden
 
+        def quantize_hidden(q):
+            words = codes.tile([P, PAIR], U32, name="h_words", align_bytes=64)
+            scales = codes.tile([P, PAIR], U8, name="h_scales", align_bytes=64)
+            nc.vector.quantize_mx(out=words[:].bitcast(FP8X4), scales=scales[:], in_=hidden_of[q][:])
+            h_codes[q] = (words, scales)
+
+        def layer_two(q):
+            w2_words, w2_scales = w2_codes[q]
+            h_words, h_scales = h_codes[q]
             y_bank = psum.tile([P, 2, PAIR], F32, name="y_bank")
             for b in range(2):
                 for i in range(2):
@@ -148,10 +192,33 @@ def tile_routed_moe_kernel(tc, xT, w1, w2, gate, offs, out):
                         start=True,
                         stop=True,
                     )
-            for b in range(2):
-                gated = codes.tile([P, PAIR], F32, name="gated")
-                nc.vector.tensor_tensor(gated[:], y_bank[:, b, :], gates[:, slots], MULT)
-                nc.vector.tensor_copy(windows[b][:].indirect(index_cols), gated[:])
+            sums = sums_pool.tile([P, 2, PAIR], F32, name="sums")
+            nc.scalar.activation(out=sums[:], in_=y_bank[:], func=IDENTITY, bias=zero_of(2 * q + 4))
+            sums_of[q] = sums
 
-        for b in range(2):
-            nc.sync.dma_start(out=out[P * b : P * (b + 1), :], in_=windows[b][:])
+        def scatter(q, b):
+            index_cols = offsets[:, PAIR // 16 * q : PAIR // 16 * (q + 1)]
+            nc.vector.tensor_tensor(windows[b][:].indirect(index_cols), sums_of[q][:, b, :], gates[:, PAIR * q : PAIR * (q + 1)], MULT)
+
+        def scatter_pair(q):
+            scatter(q, 0)
+            if q == PAIRS - 1:
+                nc.sync.dma_start(out=out[0:P, :], in_=windows[0][:])
+            scatter(q, 1)
+
+        stages = (
+            (quantize_hidden, 3),
+            (scatter_pair, 4),
+            (layer_one, 2),
+            (quantize_w2, 1),
+            (convert_w1, 0),
+            (gather_tokens, 1),
+            (layer_two, 3),
+            (quantize_w1, 1),
+            (convert_w2, 0),
+        )
+        for step in range(PAIRS + 4):
+            for run, lag in stages:
+                if 0 <= step - lag < PAIRS:
+                    run(step - lag)
+        nc.sync.dma_start(out=out[P:N, :], in_=windows[1][:])

from contextlib import ExitStack

import concourse.mybir as mybir
from concourse.masks import make_identity

K, T, E, C, H, N = 512, 2048, 16, 128, 512, 256
FLOPS = 2 * E * C * (K * H + H * N)
GATE_ROWS = 8
BYTES = 4 * (K * T + E * K * H + E * H * N + N * T + GATE_ROWS * E * C) + 2 * 128 * (E * C // 16)

F32 = mybir.dt.float32
BF16 = mybir.dt.bfloat16
U32 = mybir.dt.uint32
U16 = mybir.dt.uint16
U8 = mybir.dt.uint8
FP8X4 = mybir.dt.float8_e4m3fn_x4
SILU = mybir.ActivationFunctionType.Silu
IDENTITY = mybir.ActivationFunctionType.Identity
MULT = mybir.AluOpType.mult

P = 128
PACK = 4
PAIRS = E // 2
PAIR = 2 * C
X_CHUNKS = (256, 512, 512, 512, 256)
GATHERS = {0: 1, 1: 1, 2: 1, 3: 1, 4: 2, 6: 2}
W1_PIECES = (64, 32, 32)


def tile_routed_moe_kernel(tc, xT, w1, w2, gate, offs, out):
    nc = tc.nc
    with ExitStack() as ctx:
        keep = ctx.enter_context(tc.tile_pool(name="keep", bufs=1))
        raws = ctx.enter_context(tc.tile_pool(name="raws", bufs=12))
        stage = ctx.enter_context(tc.tile_pool(name="stage", bufs=4))
        codes = ctx.enter_context(tc.tile_pool(name="codes", bufs=3))
        sums_pool = ctx.enter_context(tc.tile_pool(name="sums_pool", bufs=3))
        psum = ctx.enter_context(tc.psum_pool(name="psum", bufs=3))
        gate_psum = ctx.enter_context(tc.psum_pool(name="gate_psum", bufs=2))

        offsets = keep.tile([P, T // 16], U16, name="offsets")
        x_words = keep.tile([P, T], U32, name="x_words", align_bytes=64)
        x_scales = keep.tile([P, T], U8, name="x_scales", align_bytes=64)
        gate_rows = keep.tile([P, C], F32, name="gate_rows")
        gates = keep.tile([P, E * C], F32, name="gates")
        ident = keep.tile([P, P], F32, name="ident")
        zeros = keep.tile([P, 2 * E], F32, name="zeros")
        window0 = keep.tile([P, T], F32, name="window0")
        window1 = keep.tile([P, T], F32, name="window1")
        windows = [window0, window1]

        nc.vector.memset(zeros[:, 0:1], 0.0)
        nc.scalar.activation(out=zeros[:, 1:2], in_=zeros[:, 0:1], func=SILU)
        nc.gpsimd.memset(x_scales[:], 0)
        make_identity(nc, ident[:])

        xT_rows = xT.rearrange("(p j) t -> p j t", j=PACK)
        x_raw = []
        start = 0
        for k, width in enumerate(X_CHUNKS):
            raw = raws.tile([P, PACK, width], F32, name="x_raw", tag="raw")
            nc.sync.dma_start(out=raw[:], in_=xT_rows[:, :, start : start + width])
            x_raw.append(raw)
            start += width
            if k == 0:
                nc.sync.dma_start(out=gate_rows[:], in_=gate[0:GATE_ROWS, :].rearrange("r (e c) -> (r e) c", c=C))
            if k == 1:
                nc.sync.dma_start(offsets[:], offs)

        start = 0
        for k, width in enumerate(X_CHUNKS):
            cols = slice(start, start + width)
            start += width
            grouped = stage.tile([P, width * PACK], BF16, name="x_grouped", align_bytes=64)
            dst = grouped[:].rearrange("p (c i j) -> p c j i", i=4, j=PACK)
            src = x_raw[k][:].rearrange("p j (c i) -> p c j i", i=4)
            cut = (width // 4) * 3 // 4
            nc.vector.tensor_copy(out=dst[:, :cut], in_=src[:, :cut])
            nc.scalar.copy(out=dst[:, cut:], in_=src[:, cut:])
            nc.vector.quantize_mx(out=x_words[:, cols].bitcast(FP8X4), scales=x_scales[:, cols], in_=grouped[:])

        for quad in range(E // 4):
            bank = gate_psum.tile([P, 4, C], F32, name="gate_bank")
            for i in range(4):
                e = 4 * quad + i
                nc.tensor.matmul(bank[:, i, :], ident[:, e : e + 1].to_broadcast([P, P]), gate_rows[:], start=True, stop=True)
            nc.scalar.copy(out=gates[:, 4 * C * quad : 4 * C * (quad + 1)], in_=bank[:].rearrange("p i c -> p (i c)"))

        w1_grouped, w2_grouped, w1_codes, w2_codes = {}, {}, {}, {}
        slot_codes, hidden_of, h_codes, sums_of = {}, {}, {}, {}

        def zero_of(e):
            return zeros[:, E + e : E + e + 1] if e < E else 0.0

        def convert_w1(q):
            for e in (2 * q, 2 * q + 1):
                raw = raws.tile([P, PACK, H], F32, name="w1_raw", tag="raw")
                nc.sync.dma_start(out=raw[:], in_=w1[e].rearrange("(p j) i -> p j i", j=PACK))
                grouped = stage.tile([P, H * PACK], BF16, name="w1_grouped", align_bytes=64)
                dst = grouped[:].rearrange("p (t m j) -> p m j t", t=4, j=PACK)
                src = raw[:].rearrange("p j (m t) -> p m j t", t=4)
                m = 0
                for k, width in enumerate(W1_PIECES):
                    nc.scalar.copy(out=dst[:, m : m + width], in_=src[:, m : m + width])
                    m += width
                    if k == 1:
                        nc.scalar.mul(zeros[:, E + e : E + e + 1], grouped[:, 0:1], 0.0)
                w1_grouped[e] = grouped

        def convert_w2(q):
            raw = raws.tile([P, 2, PACK, N], F32, name="w2_raw", tag="raw")
            nc.sync.dma_start(out=raw[:], in_=w2[2 * q : 2 * q + 2].rearrange("e (p j) n -> p e j n", j=PACK))
            grouped = stage.tile([P, 2 * N * PACK], BF16, name="w2_grouped", align_bytes=64, bufs=1)
            dst = grouped[:].rearrange("p (e c i j) -> p e c j i", e=2, i=4, j=PACK)
            src = raw[:].rearrange("p e j (c i) -> p e c j i", i=4)
            for i in range(2):
                nc.vector.tensor_copy(out=dst[:, i], in_=src[:, i])
            w2_grouped[q] = grouped

        def quantize_w1(q):
            for e in (2 * q, 2 * q + 1):
                words = codes.tile([P, H], U32, name="w1_words", align_bytes=64)
                scales = codes.tile([P, H], U8, name="w1_scales", align_bytes=64)
                nc.vector.quantize_mx(out=words[:].bitcast(FP8X4), scales=scales[:], in_=w1_grouped[e][:])
                w1_codes[e] = (words, scales)

        def quantize_w2(q):
            words = codes.tile([P, 2 * N], U32, name="w2_words", align_bytes=64)
            scales = codes.tile([P, 2 * N], U8, name="w2_scales", align_bytes=64)
            nc.vector.quantize_mx(out=words[:].bitcast(FP8X4), scales=scales[:], in_=w2_grouped[q][:])
            w2_codes[q] = (words, scales)

        def gather_tokens(q):
            if q not in GATHERS:
                return
            n = GATHERS[q]
            index_cols = offsets[:, PAIR // 16 * q : PAIR // 16 * (q + n)]
            words = codes.tile([P, n * PAIR], U32, name="slot_words", align_bytes=64, bufs=4)
            scales = codes.tile([P, n * PAIR], U8, name="slot_scales", align_bytes=64, bufs=4)
            nc.vector.tensor_copy(words[:], x_words[:].indirect(index_cols))
            nc.vector.tensor_copy(scales[:], x_scales[:].indirect(index_cols))
            for k in range(n):
                slot_codes[q + k] = (words, scales, PAIR * k)

        def layer_one(q):
            slot_words, slot_scales, base = slot_codes[q]
            hidden = stage.tile([P, PAIR * PACK], BF16, name="hidden", align_bytes=64, bufs=2)
            for i in range(2):
                e = 2 * q + i
                words, scales = w1_codes[e]
                mine = slice(base + C * i, base + C * (i + 1))
                h_bank = psum.tile([P, 4, C], F32, name="h_bank")
                for t in range(4):
                    rows = slice(P * t, P * (t + 1))
                    nc.tensor.matmul_mx(
                        out=h_bank[:, t, :],
                        lhsT=words[:, rows].bitcast(FP8X4),
                        lhsT_scale=scales[:, rows],
                        rhs=slot_words[:, mine].bitcast(FP8X4),
                        rhs_scale=slot_scales[:, mine],
                        start=True,
                        stop=True,
                    )
                nc.scalar.activation(
                    out=hidden[:, PACK * C * i : PACK * C * (i + 1)].rearrange("p (c t) -> p c t", t=PACK),
                    in_=h_bank[:].rearrange("p t c -> p c t"),
                    func=SILU,
                    bias=zero_of(e + 1),
                )
            hidden_of[q] = hidden

        def quantize_hidden(q):
            words = codes.tile([P, PAIR], U32, name="h_words", align_bytes=64)
            scales = codes.tile([P, PAIR], U8, name="h_scales", align_bytes=64)
            nc.vector.quantize_mx(out=words[:].bitcast(FP8X4), scales=scales[:], in_=hidden_of[q][:])
            h_codes[q] = (words, scales)

        def layer_two(q):
            w2_words, w2_scales = w2_codes[q]
            h_words, h_scales = h_codes[q]
            y_bank = psum.tile([P, 2, PAIR], F32, name="y_bank")
            for b in range(2):
                for i in range(2):
                    mine = slice(C * i, C * (i + 1))
                    rows = slice(N * i + P * b, N * i + P * (b + 1))
                    nc.tensor.matmul_mx(
                        out=y_bank[:, b, mine],
                        lhsT=w2_words[:, rows].bitcast(FP8X4),
                        lhsT_scale=w2_scales[:, rows],
                        rhs=h_words[:, mine].bitcast(FP8X4),
                        rhs_scale=h_scales[:, mine],
                        start=True,
                        stop=True,
                    )
            sums = sums_pool.tile([P, 2, PAIR], F32, name="sums")
            nc.scalar.activation(out=sums[:], in_=y_bank[:], func=IDENTITY, bias=zero_of(2 * q + 4))
            sums_of[q] = sums

        def scatter(q, b):
            index_cols = offsets[:, PAIR // 16 * q : PAIR // 16 * (q + 1)]
            nc.vector.tensor_tensor(windows[b][:].indirect(index_cols), sums_of[q][:, b, :], gates[:, PAIR * q : PAIR * (q + 1)], MULT)

        def scatter_pair(q):
            scatter(q, 0)
            if q == PAIRS - 1:
                nc.sync.dma_start(out=out[0:P, :], in_=windows[0][:])
            scatter(q, 1)

        stages = (
            (quantize_hidden, 3),
            (scatter_pair, 4),
            (layer_one, 2),
            (quantize_w2, 1),
            (convert_w1, 0),
            (gather_tokens, 1),
            (layer_two, 3),
            (quantize_w1, 1),
            (convert_w2, 0),
        )
        for step in range(PAIRS + 4):
            for run, lag in stages:
                if 0 <= step - lag < PAIRS:
                    run(step - lag)
        nc.sync.dma_start(out=out[P:N, :], in_=windows[1][:])
